import numpy as np
import ml_dtypes


def mxq(x, axis, fmt="e4m3"):
    dtype, down = {"e4m3": (ml_dtypes.float8_e4m3fn, 7), "e5m2": (ml_dtypes.float8_e5m2, 14)}[fmt]
    v = np.moveaxis(np.asarray(x, np.float32).astype(ml_dtypes.bfloat16).astype(np.float64), axis, -1)
    blocks = v.reshape(v.shape[:-1] + (-1, 32))
    amax = np.abs(blocks).max(-1, keepdims=True)
    byte = np.maximum(np.where(amax > 0, np.frexp(amax)[1] - 1 + 127, 0) - down, 1)
    scale = np.exp2(byte - 127.0)
    codes = (blocks / scale).astype(np.float32).astype(dtype).astype(np.float64)
    return np.moveaxis((codes * scale).reshape(v.shape), -1, axis)


WIDE = False


def mx_kscale(k):
    if not WIDE:
        return np.ones(k)
    levels = np.array([10, -10, 5, -5, 0])
    if k % 512:
        return np.exp2(np.random.permutation(np.resize(levels, k // 32))).repeat(32)
    a = np.empty((k // 512, 16))
    for p in range(k // 512):
        a[p, :8] = np.random.permutation(np.resize(levels, 8))
        for g in range(8):
            far = levels[np.abs(levels - a[p, g]) >= 10]
            a[p, g + 8] = far[np.random.randint(len(far))]
    return np.exp2(a.ravel()).repeat(32)


def f64(x):
    return np.asarray(x).astype(np.float64)


def striped8(idx):
    return np.concatenate([v.reshape(-1, 16).T for v in idx]).astype(np.uint16)


def unstriped8(offs):
    return np.stack([offs[16 * g:16 * g + 16].T.reshape(-1) for g in range(8)]).astype(np.int64)


E2M1 = np.array([0.0, 0.5, 1.0, 1.5, 2.0, 3.0, 4.0, 6.0, -0.0, -0.5, -1.0, -1.5, -2.0, -3.0, -4.0, -6.0])


def pack_weight(w, fmt):
    k, n = w.shape
    w = f64(np.asarray(w, np.float32).astype(ml_dtypes.bfloat16)).reshape(k // 32, 32, n)
    amax = np.abs(w).max(1)
    if fmt == "e4m3":
        byte = np.frexp(amax)[1] - 1 + 127 - 7
    else:
        mant, ex = np.frexp(amax / 6.0)
        byte = np.where(mant > 0.5, ex, ex - 1) + 127
    byte = np.clip(np.where(amax > 0, byte, 1), 1, 254)
    scaled = (w * np.exp2(127.0 - byte)[:, None, :]).reshape(k, n).astype(np.float32)
    by_word = np.ascontiguousarray(scaled.reshape(k // 512, 128, 4, n).transpose(0, 1, 3, 2))
    if fmt == "e4m3":
        words = by_word.astype(ml_dtypes.float8_e4m3fn).view(np.uint8)
    else:
        c = by_word.astype(ml_dtypes.float4_e2m1fn).view(np.uint8) & 0xF
        words = (c[..., 0::2] | (c[..., 1::2] << 4)).reshape(k // 512, 128, 2 * n)
    return np.ascontiguousarray(words), np.ascontiguousarray(byte.astype(np.uint8).reshape(k // 512, 16, n))


def unpack_weight(words, scales, fmt):
    g, _, n = scales.shape
    words = np.ascontiguousarray(words).reshape(g, 128, n, -1)
    if fmt == "e4m3":
        vals = words.view(ml_dtypes.float8_e4m3fn).astype(np.float64)
    else:
        nib = np.empty((g, 128, n, 4), np.uint8)
        nib[..., 0::2] = words & 0xF
        nib[..., 1::2] = words >> 4
        vals = E2M1[nib]
    vals = vals * np.repeat(np.exp2(scales.astype(np.float64) - 127.0), 8, axis=1)[..., None]
    return vals.transpose(0, 1, 3, 2).reshape(g * 512, n)


K, L, M, T, S = 512, 1536, 128, 2048, 512


def setup_inputs():
    n = np.random.standard_normal
    s1 = mx_kscale(K)[:, None]
    s2 = mx_kscale(L)[:, None]
    p_w4 = pack_weight(n((K, M)) / np.sqrt(K) / s1, "e2m1")
    return {
        "xT": (n((K, T)) * s1).astype(np.float32),
        "w4_words": p_w4[0],
        "w4_scales": p_w4[1],
        "c": (n((L, S)) * s2).astype(np.float32),
        "u": (n((L, M)) / np.sqrt(L) / s2).astype(np.float32),
        "wgt": np.repeat(np.random.uniform(0.5, 2.0, (8, S)), 16, axis=0).astype(np.float32),
        "offs": striped8(np.stack([np.random.permutation(T)[:S] for _ in range(8)])),
    }


def reference(xT, w4_words, w4_scales, c, u, wgt, offs):
    idx = unstriped8(offs)
    group = np.arange(K) % 512 // 64
    xg = f64(wgt)[np.arange(K) // 4 % 128] * f64(xT)[np.arange(K)[:, None], idx[group]]
    xT_ = mxq(xg, 0, "e4m3")
    w4_ = unpack_weight(w4_words, w4_scales, "e2m1")
    c_ = mxq(f64(c), 0, "e4m3")
    u_ = mxq(f64(u), 0, "e4m3")
    y = w4_.T @ xT_ + u_.T @ c_
    return y

@@ -1,0 +1,158 @@
+from contextlib import ExitStack
+
+import concourse.mybir as mybir
+
+FLOPS = 268435456
+
+F32 = mybir.dt.float32
+BF16 = mybir.dt.bfloat16
+I32 = mybir.dt.int32
+U32 = mybir.dt.uint32
+U16 = mybir.dt.uint16
+U8 = mybir.dt.uint8
+E4M3 = mybir.dt.float8_e4m3fn_x4
+E2M1 = mybir.dt.float4_e2m1fn_x4
+MULT = mybir.AluOpType.mult
+
+P = 128
+J = 4
+M = 128
+T = 2048
+S = 512
+DENSE = 3
+GROUP = 128
+PIECE = 256
+
+
+def interleave(copy, dst, src):
+    copy(
+        dst.rearrange("p (c i t) -> p c t i", i=4, t=J),
+        src.rearrange("p t (c i) -> p c t i", i=4),
+    )
+
+
+def tile_list_hmix_none_kernel(tc, xT, w4_words, w4_scales, c, u, wgt, offs, out):
+    nc = tc.nc
+    with ExitStack() as ctx:
+        lists = ctx.enter_context(tc.tile_pool(name="lists", bufs=1))
+        keep = ctx.enter_context(tc.tile_pool(name="keep", bufs=1))
+        psum = ctx.enter_context(tc.psum_pool(name="psum", bufs=1))
+
+        offs_sb = lists.tile([P, S // 16], U16, name="offs_sb")
+        wgt_sb = keep.tile([P, S], F32, name="wgt_sb")
+        w4_sb = keep.tile([P, 2 * M], U8, name="w4_sb", align_bytes=64)
+        w4_sc = keep.tile([P, M], U8, name="w4_sc", align_bytes=64)
+        u_raw = keep.tile([P, DENSE, J * M], F32, name="u_raw")
+        xt = [keep.tile([P, T], F32, name="xt%d" % t) for t in range(J)]
+        splits = [[(0, 512)], [(0, 512)], [(0, 256), (256, 384), (384, 512)]]
+        c_raw = [
+            [keep.tile([P, J, hi - lo], F32, name="c_raw%d_%d" % (a, lo)) for lo, hi in splits[a]]
+            for a in range(DENSE)
+        ]
+
+        nc.vector.memset(w4_sc[:].bitcast(I32), 0)
+
+        x_planes = xT.rearrange("(p j) t -> j p t", j=J)
+        nc.sync.dma_start(offs_sb[:], offs)
+        nc.sync.dma_start(out=wgt_sb[:], in_=wgt)
+        nc.sync.dma_start(out=xt[0][:], in_=x_planes[0])
+        nc.sync.dma_start(out=w4_sb[:].bitcast(I32), in_=w4_words[0].bitcast(I32))
+        for q in range(4):
+            nc.sync.dma_start(
+                out=w4_sc[32 * q : 32 * q + 4, :].bitcast(I32),
+                in_=w4_scales[0, 4 * q : 4 * q + 4, :].bitcast(I32),
+            )
+        nc.scalar.dma_start(out=xt[1][:], in_=x_planes[1])
+        nc.sync.dma_start(out=u_raw[:], in_=u.rearrange("(a p j) n -> p a (j n)", p=P, j=J))
+        nc.sync.dma_start(out=xt[2][:], in_=x_planes[2])
+        nc.scalar.dma_start(out=xt[3][:], in_=x_planes[3])
+        c_rows = c.rearrange("(a p j) n -> a p j n", p=P, j=J)
+        for a in range(DENSE):
+            for k, (lo, hi) in enumerate(splits[a]):
+                dst, src = c_raw[a][k][:], c_rows[a, :, :, lo:hi]
+                if hi - lo == S:
+                    dst, src = dst.rearrange("p j n -> p (j n)"), src.rearrange("p j n -> p (j n)")
+                nc.sync.dma_start(out=dst, in_=src)
+
+        u_codes = keep.tile([P, DENSE, M], U32, name="u_codes", align_bytes=64)
+        u_scales = keep.tile([P, DENSE, M], U8, name="u_scales", align_bytes=64)
+        u_bf = keep.tile([P, DENSE, M * J], BF16, name="u_bf", align_bytes=64)
+        for a in range(DENSE):
+            interleave(nc.vector.tensor_copy, u_bf[:, a, :], u_raw[:, a, :].rearrange("p (j n) -> p j n", j=J))
+        for a in range(DENSE):
+            nc.vector.quantize_mx(out=u_codes[:, a, :].bitcast(E4M3), scales=u_scales[:, a, :], in_=u_bf[:, a, :])
+
+        halves = S // PIECE
+        picked = [keep.tile([P, J, PIECE], F32, name="picked%d" % h) for h in range(halves)]
+        for t in range(J):
+            for h in range(halves):
+                nc.vector.tensor_tensor(
+                    picked[h][:, t, :],
+                    xt[t][:].indirect(offs_sb[:, h * PIECE // 16 : (h + 1) * PIECE // 16]),
+                    wgt_sb[:, h * PIECE : (h + 1) * PIECE],
+                    MULT,
+                )
+
+        x_codes = keep.tile([P, S], U32, name="x_codes", align_bytes=64)
+        x_scales = keep.tile([P, S], U8, name="x_scales", align_bytes=64)
+        x_bf = [keep.tile([P, PIECE * J], BF16, name="x_bf%d" % h, align_bytes=64) for h in range(halves)]
+        for h in range(halves):
+            interleave(nc.scalar.copy, x_bf[h][:], picked[h][:])
+        for h in range(halves):
+            cols = slice(h * PIECE, (h + 1) * PIECE)
+            nc.vector.quantize_mx(out=x_codes[:, cols].bitcast(E4M3), scales=x_scales[:, cols], in_=x_bf[h][:])
+
+        groups = S // GROUP
+        acc = [psum.tile([M, GROUP], F32, name="acc%d" % g) for g in range(groups)]
+        for g in range(groups):
+            cols = slice(g * GROUP, (g + 1) * GROUP)
+            nc.tensor.matmul_mx(
+                out=acc[g][:],
+                lhsT=w4_sb[:].bitcast(E2M1),
+                lhsT_scale=w4_sc[:],
+                rhs=x_codes[:, cols].bitcast(E4M3),
+                rhs_scale=x_scales[:, cols],
+                start=True,
+                stop=False,
+            )
+
+        c_codes = [keep.tile([P, S], U32, name="c_codes%d" % a, align_bytes=64) for a in range(DENSE)]
+        c_scales = [keep.tile([P, S], U8, name="c_scales%d" % a, align_bytes=64) for a in range(DENSE)]
+        c_bf = [keep.tile([P, S * J], BF16, name="c_bf%d" % a, align_bytes=64) for a in range(DENSE)]
+        res = [keep.tile([M, GROUP], F32, name="res%d" % g) for g in range(groups)]
+        vec, sca = nc.vector.tensor_copy, nc.scalar.copy
+        pieces = [
+            (0, 0, (0, 256), [(0, 256, vec)]),
+            (0, 0, (256, 512), [(256, 512, sca)]),
+            (1, 0, (0, 256), [(0, 256, vec)]),
+            (1, 0, (256, 512), [(256, 512, sca)]),
+            (2, 0, (0, 128), [(0, 128, vec)]),
+            (2, 0, (128, 256), [(128, 256, sca)]),
+            (2, 1, (256, 384), [(256, 384, sca)]),
+            (2, 2, (384, 512), [(384, 448, vec), (448, 512, vec)]),
+        ]
+        for a, k, (lo, hi), shares in pieces:
+            base = splits[a][k][0]
+            for s_lo, s_hi, copy in shares:
+                interleave(copy, c_bf[a][:, s_lo * J : s_hi * J], c_raw[a][k][:, :, s_lo - base : s_hi - base])
+            cuts = [(lo, hi)] if len(shares) == 1 else [(s_lo, s_hi) for s_lo, s_hi, copy in shares]
+            for q_lo, q_hi in cuts:
+                nc.vector.quantize_mx(
+                    out=c_codes[a][:, q_lo:q_hi].bitcast(E4M3),
+                    scales=c_scales[a][:, q_lo:q_hi],
+                    in_=c_bf[a][:, q_lo * J : q_hi * J],
+                )
+            for g in range(lo // GROUP, hi // GROUP):
+                cols = slice(g * GROUP, (g + 1) * GROUP)
+                nc.tensor.matmul_mx(
+                    out=acc[g][:],
+                    lhsT=u_codes[:, a, :].bitcast(E4M3),
+                    lhsT_scale=u_scales[:, a, :],
+                    rhs=c_codes[a][:, cols].bitcast(E4M3),
+                    rhs_scale=c_scales[a][:, cols],
+                    start=False,
+                    stop=(a == DENSE - 1),
+                )
+                if a == DENSE - 1:
+                    (vec if g == groups - 1 else sca)(res[g][:], acc[g][:])
+                    nc.sync.dma_start(out=out[:, cols], in_=res[g][:])

@@ -39,7 +39,10 @@ def tile_list_hmix_none_kernel(tc, xT, w4_words, w4_scales, c, u, wgt, offs, out
         psum = ctx.enter_context(tc.psum_pool(name="psum", bufs=1))
 
         offs_sb = lists.tile([P, S // 16], U16, name="offs_sb")
-        wgt_sb = keep.tile([P, S], F32, name="wgt_sb")
+        wgt_sb = keep.tile([P, S], F32, name="wgt_sb", align_bytes=64)
+        wgt_cut = keep.tile([P, 32], F32, name="wgt_cut", align_bytes=64)
+        wgt_turned = keep.tile([P, 32], F32, name="wgt_turned", align_bytes=64)
+        wgt_wide = keep.tile([P, S], F32, name="wgt_wide", align_bytes=64)
         w4_sb = keep.tile([P, 2 * M], U8, name="w4_sb", align_bytes=64)
         w4_sc = keep.tile([P, M], U8, name="w4_sc", align_bytes=64)
         u_raw = keep.tile([P, DENSE, J * M], F32, name="u_raw")
@@ -54,7 +57,7 @@ def tile_list_hmix_none_kernel(tc, xT, w4_words, w4_scales, c, u, wgt, offs, out
 
         x_planes = xT.rearrange("(p j) t -> j p t", j=J)
         nc.sync.dma_start(offs_sb[:], offs)
-        nc.sync.dma_start(out=wgt_sb[:], in_=wgt)
+        nc.sync.dma_start(out=wgt_cut[:], in_=wgt.rearrange("(g r) (b c) -> r g b c", r=16, c=32)[0])
         nc.sync.dma_start(out=xt[0][:], in_=x_planes[0])
         nc.sync.dma_start(out=w4_sb[:].bitcast(I32), in_=w4_words[0].bitcast(I32))
         for q in range(4):
@@ -73,6 +76,13 @@ def tile_list_hmix_none_kernel(tc, xT, w4_words, w4_scales, c, u, wgt, offs, out
                 if hi - lo == S:
                     dst, src = dst.rearrange("p j n -> p (j n)"), src.rearrange("p j n -> p (j n)")
                 nc.sync.dma_start(out=dst, in_=src)
+
+        nc.vector.transpose(wgt_turned[:], wgt_cut[:])
+        nc.vector.tensor_copy(
+            wgt_wide[:].rearrange("p (b h r) -> p b h r", h=2, r=16),
+            wgt_turned[:].rearrange("p (h b o) -> p b h o", h=2, o=1).to_broadcast([P, 16, 2, 16]),
+        )
+        nc.vector.transpose(wgt_sb[:], wgt_wide[:])
 
         u_codes = keep.tile([P, DENSE, M], U32, name="u_codes", align_bytes=64)
         u_scales = keep.tile([P, DENSE, M], U8, name="u_scales", align_bytes=64)

@@ -37,6 +37,7 @@ def tile_list_hmix_none_kernel(tc, xT, w4_words, w4_scales, c, u, wgt, offs, out
         lists = ctx.enter_context(tc.tile_pool(name="lists", bufs=1))
         keep = ctx.enter_context(tc.tile_pool(name="keep", bufs=1))
         psum = ctx.enter_context(tc.psum_pool(name="psum", bufs=1))
+        vec, sca = nc.vector.tensor_copy, nc.scalar.copy
 
         offs_sb = lists.tile([P, S // 16], U16, name="offs_sb")
         wgt_sb = keep.tile([P, S], F32, name="wgt_sb", align_bytes=64)
@@ -45,40 +46,38 @@ def tile_list_hmix_none_kernel(tc, xT, w4_words, w4_scales, c, u, wgt, offs, out
         wgt_wide = keep.tile([P, S], F32, name="wgt_wide", align_bytes=64)
         w4_sb = keep.tile([P, 2 * M], U8, name="w4_sb", align_bytes=64)
         w4_sc = keep.tile([P, M], U8, name="w4_sc", align_bytes=64)
-        u_raw = keep.tile([P, DENSE, J * M], F32, name="u_raw")
         xt = [keep.tile([P, T], F32, name="xt%d" % t) for t in range(J)]
         splits = [[(0, 512)], [(0, 512)], [(0, 256), (256, 384), (384, 512)]]
-        c_raw = [
-            [keep.tile([P, J, hi - lo], F32, name="c_raw%d_%d" % (a, lo)) for lo, hi in splits[a]]
+        c_raw = {
+            (a, lo): keep.tile([P, J, hi - lo], F32, name="c_raw%d_%d" % (a, lo))
             for a in range(DENSE)
-        ]
-
-        nc.vector.memset(w4_sc[:].bitcast(I32), 0)
+            for lo, hi in splits[a]
+        }
+        u_raw = keep.tile([P, DENSE, J * M], F32, name="u_raw")
 
         x_planes = xT.rearrange("(p j) t -> j p t", j=J)
+        c_rows = c.rearrange("(a p j) n -> a p j n", p=P, j=J)
+        u_rows = u.rearrange("(a p j) n -> p a (j n)", p=P, j=J)
+        nc.vector.memset(w4_sc[:].bitcast(I32), 0)
+        nc.sync.dma_start(out=xt[0][:], in_=x_planes[0])
         nc.sync.dma_start(offs_sb[:], offs)
         nc.sync.dma_start(out=wgt_cut[:], in_=wgt.rearrange("(g r) (b c) -> r g b c", r=16, c=32)[0])
-        nc.sync.dma_start(out=xt[0][:], in_=x_planes[0])
+        nc.sync.dma_start(out=xt[1][:], in_=x_planes[1])
+        nc.sync.dma_start(out=u_raw[:], in_=u_rows)
+        nc.sync.dma_start(out=xt[2][:], in_=x_planes[2])
+        nc.sync.dma_start(out=xt[3][:], in_=x_planes[3])
         nc.sync.dma_start(out=w4_sb[:].bitcast(I32), in_=w4_words[0].bitcast(I32))
         for q in range(4):
             nc.sync.dma_start(
                 out=w4_sc[32 * q : 32 * q + 4, :].bitcast(I32),
                 in_=w4_scales[0, 4 * q : 4 * q + 4, :].bitcast(I32),
             )
-        nc.scalar.dma_start(out=xt[1][:], in_=x_planes[1])
-        nc.sync.dma_start(out=u_raw[:], in_=u.rearrange("(a p j) n -> p a (j n)", p=P, j=J))
-        nc.sync.dma_start(out=xt[2][:], in_=x_planes[2])
-        nc.scalar.dma_start(out=xt[3][:], in_=x_planes[3])
-        c_rows = c.rearrange("(a p j) n -> a p j n", p=P, j=J)
         for a in range(DENSE):
-            for k, (lo, hi) in enumerate(splits[a]):
-                dst, src = c_raw[a][k][:], c_rows[a, :, :, lo:hi]
-                if hi - lo == S:
-                    dst, src = dst.rearrange("p j n -> p (j n)"), src.rearrange("p j n -> p (j n)")
-                nc.sync.dma_start(out=dst, in_=src)
+            for lo, hi in splits[a]:
+                nc.sync.dma_start(out=c_raw[a, lo][:], in_=c_rows[a, :, :, lo:hi])
 
         nc.vector.transpose(wgt_turned[:], wgt_cut[:])
-        nc.vector.tensor_copy(
+        vec(
             wgt_wide[:].rearrange("p (b h r) -> p b h r", h=2, r=16),
             wgt_turned[:].rearrange("p (h b o) -> p b h o", h=2, o=1).to_broadcast([P, 16, 2, 16]),
         )
@@ -88,7 +87,7 @@ def tile_list_hmix_none_kernel(tc, xT, w4_words, w4_scales, c, u, wgt, offs, out
         u_scales = keep.tile([P, DENSE, M], U8, name="u_scales", align_bytes=64)
         u_bf = keep.tile([P, DENSE, M * J], BF16, name="u_bf", align_bytes=64)
         for a in range(DENSE):
-            interleave(nc.vector.tensor_copy, u_bf[:, a, :], u_raw[:, a, :].rearrange("p (j n) -> p j n", j=J))
+            interleave(sca, u_bf[:, a, :], u_raw[:, a, :].rearrange("p (j n) -> p j n", j=J))
         for a in range(DENSE):
             nc.vector.quantize_mx(out=u_codes[:, a, :].bitcast(E4M3), scales=u_scales[:, a, :], in_=u_bf[:, a, :])
 
@@ -107,8 +106,8 @@ def tile_list_hmix_none_kernel(tc, xT, w4_words, w4_scales, c, u, wgt, offs, out
         x_scales = keep.tile([P, S], U8, name="x_scales", align_bytes=64)
         x_bf = [keep.tile([P, PIECE * J], BF16, name="x_bf%d" % h, align_bytes=64) for h in range(halves)]
         for h in range(halves):
-            interleave(nc.scalar.copy, x_bf[h][:], picked[h][:])
-        for h in range(halves):
+            interleave((sca, vec)[h], x_bf[h][:], picked[h][:])
+        for h in reversed(range(halves)):
             cols = slice(h * PIECE, (h + 1) * PIECE)
             nc.vector.quantize_mx(out=x_codes[:, cols].bitcast(E4M3), scales=x_scales[:, cols], in_=x_bf[h][:])
 
@@ -128,41 +127,37 @@ def tile_list_hmix_none_kernel(tc, xT, w4_words, w4_scales, c, u, wgt, offs, out
 
         c_codes = [keep.tile([P, S], U32, name="c_codes%d" % a, align_bytes=64) for a in range(DENSE)]
         c_scales = [keep.tile([P, S], U8, name="c_scales%d" % a, align_bytes=64) for a in range(DENSE)]
-        c_bf = [keep.tile([P, S * J], BF16, name="c_bf%d" % a, align_bytes=64) for a in range(DENSE)]
         res = [keep.tile([M, GROUP], F32, name="res%d" % g) for g in range(groups)]
-        vec, sca = nc.vector.tensor_copy, nc.scalar.copy
-        pieces = [
-            (0, 0, (0, 256), [(0, 256, vec)]),
-            (0, 0, (256, 512), [(256, 512, sca)]),
-            (1, 0, (0, 256), [(0, 256, vec)]),
-            (1, 0, (256, 512), [(256, 512, sca)]),
-            (2, 0, (0, 128), [(0, 128, vec)]),
-            (2, 0, (128, 256), [(128, 256, sca)]),
-            (2, 1, (256, 384), [(256, 384, sca)]),
-            (2, 2, (384, 512), [(384, 448, vec), (448, 512, vec)]),
+        shares = [
+            [(0, 256, vec), (256, 512, sca)],
+            [(0, 256, vec), (256, 512, sca)],
+            [(0, 128, vec), (128, 256, sca), (256, 384, sca), (384, 448, vec), (448, 512, vec)],
         ]
-        for a, k, (lo, hi), shares in pieces:
-            base = splits[a][k][0]
-            for s_lo, s_hi, copy in shares:
-                interleave(copy, c_bf[a][:, s_lo * J : s_hi * J], c_raw[a][k][:, :, s_lo - base : s_hi - base])
-            cuts = [(lo, hi)] if len(shares) == 1 else [(s_lo, s_hi) for s_lo, s_hi, copy in shares]
-            for q_lo, q_hi in cuts:
+        out_copy = [sca, sca, sca, vec]
+        out_queue = [nc.sync] * 4
+        for a in range(DENSE):
+            c_bf = {}
+            for lo, hi, copy in shares[a]:
+                base = max(b for b, e in splits[a] if b <= lo)
+                c_bf[lo] = keep.tile([P, (hi - lo) * J], BF16, name="c_bf%d_%d" % (a, lo), align_bytes=64)
+                interleave(copy, c_bf[lo][:], c_raw[a, base][:, :, lo - base : hi - base])
+            done = 0
+            for lo, hi, copy in shares[a]:
                 nc.vector.quantize_mx(
-                    out=c_codes[a][:, q_lo:q_hi].bitcast(E4M3),
-                    scales=c_scales[a][:, q_lo:q_hi],
-                    in_=c_bf[a][:, q_lo * J : q_hi * J],
+                    out=c_codes[a][:, lo:hi].bitcast(E4M3), scales=c_scales[a][:, lo:hi], in_=c_bf[lo][:]
                 )
-            for g in range(lo // GROUP, hi // GROUP):
-                cols = slice(g * GROUP, (g + 1) * GROUP)
-                nc.tensor.matmul_mx(
-                    out=acc[g][:],
-                    lhsT=u_codes[:, a, :].bitcast(E4M3),
-                    lhsT_scale=u_scales[:, a, :],
-                    rhs=c_codes[a][:, cols].bitcast(E4M3),
-                    rhs_scale=c_scales[a][:, cols],
-                    start=False,
-                    stop=(a == DENSE - 1),
-                )
-                if a == DENSE - 1:
-                    (vec if g == groups - 1 else sca)(res[g][:], acc[g][:])
-                    nc.sync.dma_start(out=out[:, cols], in_=res[g][:])
+                for g in range(done, hi // GROUP):
+                    cols = slice(g * GROUP, (g + 1) * GROUP)
+                    nc.tensor.matmul_mx(
+                        out=acc[g][:],
+                        lhsT=u_codes[:, a, :].bitcast(E4M3),
+                        lhsT_scale=u_scales[:, a, :],
+                        rhs=c_codes[a][:, cols].bitcast(E4M3),
+                        rhs_scale=c_scales[a][:, cols],
+                        start=False,
+                        stop=(a == DENSE - 1),
+                    )
+                    if a == DENSE - 1:
+                        out_copy[g](res[g][:], acc[g][:])
+                        out_queue[g].dma_start(out=out[:, cols], in_=res[g][:])
+                done = hi // GROUP

@@ -47,7 +47,7 @@ def tile_list_hmix_none_kernel(tc, xT, w4_words, w4_scales, c, u, wgt, offs, out
         w4_sb = keep.tile([P, 2 * M], U8, name="w4_sb", align_bytes=64)
         w4_sc = keep.tile([P, M], U8, name="w4_sc", align_bytes=64)
         xt = [keep.tile([P, T], F32, name="xt%d" % t) for t in range(J)]
-        splits = [[(0, 512)], [(0, 512)], [(0, 256), (256, 384), (384, 512)]]
+        splits = [[(0, 512)], [(0, 256), (256, 512)], [(0, 128), (128, 256), (256, 384), (384, 512)]]
         c_raw = {
             (a, lo): keep.tile([P, J, hi - lo], F32, name="c_raw%d_%d" % (a, lo))
             for a in range(DENSE)
@@ -105,9 +105,14 @@ def tile_list_hmix_none_kernel(tc, xT, w4_words, w4_scales, c, u, wgt, offs, out
         x_codes = keep.tile([P, S], U32, name="x_codes", align_bytes=64)
         x_scales = keep.tile([P, S], U8, name="x_scales", align_bytes=64)
         x_bf = [keep.tile([P, PIECE * J], BF16, name="x_bf%d" % h, align_bytes=64) for h in range(halves)]
+        for pair in range(J // 2):
+            for h in range(halves):
+                planes = slice(2 * pair, 2 * pair + 2)
+                (vec if pair == 1 and h == 1 else sca)(
+                    x_bf[h][:].rearrange("p (c i t) -> p c t i", i=4, t=J)[:, :, planes, :],
+                    picked[h][:, planes, :].rearrange("p t (c i) -> p c t i", i=4),
+                )
         for h in range(halves):
-            interleave((sca, vec)[h], x_bf[h][:], picked[h][:])
-        for h in reversed(range(halves)):
             cols = slice(h * PIECE, (h + 1) * PIECE)
             nc.vector.quantize_mx(out=x_codes[:, cols].bitcast(E4M3), scales=x_scales[:, cols], in_=x_bf[h][:])
 
@@ -127,11 +132,11 @@ def tile_list_hmix_none_kernel(tc, xT, w4_words, w4_scales, c, u, wgt, offs, out
 
         c_codes = [keep.tile([P, S], U32, name="c_codes%d" % a, align_bytes=64) for a in range(DENSE)]
         c_scales = [keep.tile([P, S], U8, name="c_scales%d" % a, align_bytes=64) for a in range(DENSE)]
-        res = [keep.tile([M, GROUP], F32, name="res%d" % g) for g in range(groups)]
+        res = [c_raw[DENSE - 1, S - GROUP][:, g, :] for g in range(groups)]
         shares = [
             [(0, 256, vec), (256, 512, sca)],
-            [(0, 256, vec), (256, 512, sca)],
-            [(0, 128, vec), (128, 256, sca), (256, 384, sca), (384, 448, vec), (448, 512, vec)],
+            [(0, 128, vec), (128, 256, sca), (256, 384, vec), (384, 512, sca)],
+            [(0, 128, sca), (128, 256, vec), (256, 384, sca), (384, 448, vec), (448, 512, vec)],
         ]
         out_copy = [sca, sca, sca, vec]
         out_queue = [nc.sync] * 4
@@ -157,7 +162,7 @@ def tile_list_hmix_none_kernel(tc, xT, w4_words, w4_scales, c, u, wgt, offs, out
                         start=False,
                         stop=(a == DENSE - 1),
                     )
-                    if a == DENSE - 1:
-                        out_copy[g](res[g][:], acc[g][:])
-                        out_queue[g].dma_start(out=out[:, cols], in_=res[g][:])
                 done = hi // GROUP
+        for g in range(groups):
+            out_copy[g](res[g], acc[g][:])
+            out_queue[g].dma_start(out=out[:, g * GROUP : (g + 1) * GROUP], in_=res[g])

@@ -21,14 +21,19 @@ T = 2048
 S = 512
 DENSE = 3
 GROUP = 128
-PIECE = 256
+HALF = S // 2
+HEAD = 16
+SQUARE = 32
+MX_ALIGN = 64
+ROW_ALIGN = 256
 
 
-def interleave(copy, dst, src):
-    copy(
-        dst.rearrange("p (c i t) -> p c t i", i=4, t=J),
-        src.rearrange("p t (c i) -> p c t i", i=4),
-    )
+def woven(tile):
+    return tile.rearrange("p (c i t) -> p c t i", i=4, t=J)
+
+
+def by_planes(planes):
+    return planes.rearrange("p t (c i) -> p c t i", i=4)
 
 
 def tile_list_hmix_none_kernel(tc, xT, w4_words, w4_scales, c, u, wgt, offs, out):
@@ -39,21 +44,21 @@ def tile_list_hmix_none_kernel(tc, xT, w4_words, w4_scales, c, u, wgt, offs, out
         psum = ctx.enter_context(tc.psum_pool(name="psum", bufs=1))
         vec, sca = nc.vector.tensor_copy, nc.scalar.copy
 
-        offs_sb = lists.tile([P, S // 16], U16, name="offs_sb")
-        wgt_sb = keep.tile([P, S], F32, name="wgt_sb", align_bytes=64)
-        wgt_cut = keep.tile([P, 32], F32, name="wgt_cut", align_bytes=64)
-        wgt_turned = keep.tile([P, 32], F32, name="wgt_turned", align_bytes=64)
-        wgt_wide = keep.tile([P, S], F32, name="wgt_wide", align_bytes=64)
-        w4_sb = keep.tile([P, 2 * M], U8, name="w4_sb", align_bytes=64)
-        w4_sc = keep.tile([P, M], U8, name="w4_sc", align_bytes=64)
-        xt = [keep.tile([P, T], F32, name="xt%d" % t) for t in range(J)]
-        splits = [[(0, 512)], [(0, 256), (256, 512)], [(0, 128), (128, 256), (256, 384), (384, 512)]]
+        offs_sb = lists.tile([P, S // HEAD], U16, name="offs_sb")
+        wgt_sb = keep.tile([P, S], F32, name="wgt_sb", align_bytes=MX_ALIGN)
+        wgt_cut = keep.tile([P, SQUARE], F32, name="wgt_cut", align_bytes=MX_ALIGN)
+        wgt_turned = keep.tile([P, SQUARE], F32, name="wgt_turned", align_bytes=MX_ALIGN)
+        wgt_wide = keep.tile([P, S], F32, name="wgt_wide", align_bytes=MX_ALIGN)
+        w4_sb = keep.tile([P, 2 * M], U8, name="w4_sb", align_bytes=MX_ALIGN)
+        w4_sc = keep.tile([P, M], U8, name="w4_sc", align_bytes=MX_ALIGN)
+        xt = [keep.tile([P, T], F32, name="xt%d" % t, align_bytes=ROW_ALIGN) for t in range(J)]
+        c_loads = [[(lo, lo + (S >> a)) for lo in range(0, S, S >> a)] for a in range(DENSE)]
         c_raw = {
-            (a, lo): keep.tile([P, J, hi - lo], F32, name="c_raw%d_%d" % (a, lo))
+            (a, lo): keep.tile([P, J, hi - lo], F32, name="c_raw%d_%d" % (a, lo), align_bytes=ROW_ALIGN)
             for a in range(DENSE)
-            for lo, hi in splits[a]
+            for lo, hi in c_loads[a]
         }
-        u_raw = keep.tile([P, DENSE, J * M], F32, name="u_raw")
+        u_raw = keep.tile([P, DENSE, J * M], F32, name="u_raw", align_bytes=ROW_ALIGN)
 
         x_planes = xT.rearrange("(p j) t -> j p t", j=J)
         c_rows = c.rearrange("(a p j) n -> a p j n", p=P, j=J)
@@ -61,11 +66,10 @@ def tile_list_hmix_none_kernel(tc, xT, w4_words, w4_scales, c, u, wgt, offs, out
         nc.vector.memset(w4_sc[:].bitcast(I32), 0)
         nc.sync.dma_start(out=xt[0][:], in_=x_planes[0])
         nc.sync.dma_start(offs_sb[:], offs)
-        nc.sync.dma_start(out=wgt_cut[:], in_=wgt.rearrange("(g r) (b c) -> r g b c", r=16, c=32)[0])
-        nc.sync.dma_start(out=xt[1][:], in_=x_planes[1])
+        nc.sync.dma_start(out=wgt_cut[:], in_=wgt.rearrange("(g r) (b c) -> r g b c", r=HEAD, c=SQUARE)[0])
+        for t in range(1, J):
+            nc.sync.dma_start(out=xt[t][:], in_=x_planes[t])
         nc.sync.dma_start(out=u_raw[:], in_=u_rows)
-        nc.sync.dma_start(out=xt[2][:], in_=x_planes[2])
-        nc.sync.dma_start(out=xt[3][:], in_=x_planes[3])
         nc.sync.dma_start(out=w4_sb[:].bitcast(I32), in_=w4_words[0].bitcast(I32))
         for q in range(4):
             nc.sync.dma_start(
@@ -73,48 +77,44 @@ def tile_list_hmix_none_kernel(tc, xT, w4_words, w4_scales, c, u, wgt, offs, out
                 in_=w4_scales[0, 4 * q : 4 * q + 4, :].bitcast(I32),
             )
         for a in range(DENSE):
-            for lo, hi in splits[a]:
+            for lo, hi in c_loads[a]:
                 nc.sync.dma_start(out=c_raw[a, lo][:], in_=c_rows[a, :, :, lo:hi])
 
         nc.vector.transpose(wgt_turned[:], wgt_cut[:])
         vec(
-            wgt_wide[:].rearrange("p (b h r) -> p b h r", h=2, r=16),
-            wgt_turned[:].rearrange("p (h b o) -> p b h o", h=2, o=1).to_broadcast([P, 16, 2, 16]),
+            wgt_wide[:].rearrange("p (b h r) -> p b h r", h=2, r=HEAD),
+            wgt_turned[:].rearrange("p (h b o) -> p b h o", h=2, o=1).to_broadcast([P, S // SQUARE, 2, HEAD]),
         )
         nc.vector.transpose(wgt_sb[:], wgt_wide[:])
 
-        u_codes = keep.tile([P, DENSE, M], U32, name="u_codes", align_bytes=64)
-        u_scales = keep.tile([P, DENSE, M], U8, name="u_scales", align_bytes=64)
-        u_bf = keep.tile([P, DENSE, M * J], BF16, name="u_bf", align_bytes=64)
-        for a in range(DENSE):
-            interleave(sca, u_bf[:, a, :], u_raw[:, a, :].rearrange("p (j n) -> p j n", j=J))
-        for a in range(DENSE):
-            nc.vector.quantize_mx(out=u_codes[:, a, :].bitcast(E4M3), scales=u_scales[:, a, :], in_=u_bf[:, a, :])
-
-        halves = S // PIECE
-        picked = [keep.tile([P, J, PIECE], F32, name="picked%d" % h) for h in range(halves)]
+        halves = S // HALF
+        picked = [keep.tile([P, J, HALF], F32, name="picked%d" % h) for h in range(halves)]
         for t in range(J):
             for h in range(halves):
                 nc.vector.tensor_tensor(
                     picked[h][:, t, :],
-                    xt[t][:].indirect(offs_sb[:, h * PIECE // 16 : (h + 1) * PIECE // 16]),
-                    wgt_sb[:, h * PIECE : (h + 1) * PIECE],
+                    xt[t][:].indirect(offs_sb[:, h * HALF // HEAD : (h + 1) * HALF // HEAD]),
+                    wgt_sb[:, h * HALF : (h + 1) * HALF],
                     MULT,
                 )
 
-        x_codes = keep.tile([P, S], U32, name="x_codes", align_bytes=64)
-        x_scales = keep.tile([P, S], U8, name="x_scales", align_bytes=64)
-        x_bf = [keep.tile([P, PIECE * J], BF16, name="x_bf%d" % h, align_bytes=64) for h in range(halves)]
-        for pair in range(J // 2):
+        x_codes = keep.tile([P, S], U32, name="x_codes", align_bytes=MX_ALIGN)
+        x_scales = keep.tile([P, S], U8, name="x_scales", align_bytes=MX_ALIGN)
+        x_bf = [keep.tile([P, HALF * J], BF16, name="x_bf%d" % h, align_bytes=MX_ALIGN) for h in range(halves)]
+        for first, engines in ((0, (sca, sca)), (2, (sca, vec))):
             for h in range(halves):
-                planes = slice(2 * pair, 2 * pair + 2)
-                (vec if pair == 1 and h == 1 else sca)(
-                    x_bf[h][:].rearrange("p (c i t) -> p c t i", i=4, t=J)[:, :, planes, :],
-                    picked[h][:, planes, :].rearrange("p t (c i) -> p c t i", i=4),
-                )
+                engines[h](woven(x_bf[h][:])[:, :, first : first + 2, :], by_planes(picked[h][:, first : first + 2, :]))
         for h in range(halves):
-            cols = slice(h * PIECE, (h + 1) * PIECE)
+            cols = slice(h * HALF, (h + 1) * HALF)
             nc.vector.quantize_mx(out=x_codes[:, cols].bitcast(E4M3), scales=x_scales[:, cols], in_=x_bf[h][:])
+
+        u_codes = keep.tile([P, DENSE, M], U32, name="u_codes", align_bytes=MX_ALIGN)
+        u_scales = keep.tile([P, DENSE, M], U8, name="u_scales", align_bytes=MX_ALIGN)
+        u_bf = [keep.tile([P, M * J], BF16, name="u_bf%d" % a, align_bytes=MX_ALIGN) for a in range(DENSE)]
+        for a, copy in enumerate((sca, vec, sca)):
+            copy(woven(u_bf[a][:]), by_planes(u_raw[:, a, :].rearrange("p (j n) -> p j n", j=J)))
+        for a in range(DENSE):
+            nc.vector.quantize_mx(out=u_codes[:, a, :].bitcast(E4M3), scales=u_scales[:, a, :], in_=u_bf[a][:])
 
         groups = S // GROUP
         acc = [psum.tile([M, GROUP], F32, name="acc%d" % g) for g in range(groups)]
@@ -130,28 +130,28 @@ def tile_list_hmix_none_kernel(tc, xT, w4_words, w4_scales, c, u, wgt, offs, out
                 stop=False,
             )
 
-        c_codes = [keep.tile([P, S], U32, name="c_codes%d" % a, align_bytes=64) for a in range(DENSE)]
-        c_scales = [keep.tile([P, S], U8, name="c_scales%d" % a, align_bytes=64) for a in range(DENSE)]
-        res = [c_raw[DENSE - 1, S - GROUP][:, g, :] for g in range(groups)]
-        shares = [
-            [(0, 256, vec), (256, 512, sca)],
-            [(0, 128, vec), (128, 256, sca), (256, 384, vec), (384, 512, sca)],
-            [(0, 128, sca), (128, 256, vec), (256, 384, sca), (384, 448, vec), (448, 512, vec)],
-        ]
-        out_copy = [sca, sca, sca, vec]
-        out_queue = [nc.sync] * 4
+        c_codes = [keep.tile([P, S], U32, name="c_codes%d" % a, align_bytes=MX_ALIGN) for a in range(DENSE)]
+        c_scales = [keep.tile([P, S], U8, name="c_scales%d" % a, align_bytes=MX_ALIGN) for a in range(DENSE)]
+        shares = []
+        for a in range(DENSE):
+            shares.append([])
+            for i, (lo, hi) in enumerate(c_loads[a]):
+                if a < DENSE - 1 or hi == S:
+                    mid = (lo + hi) // 2
+                    shares[a].extend([(lo, mid, vec), (mid, hi, sca)])
+                else:
+                    shares[a].append((lo, hi, (sca, vec)[i % 2]))
         for a in range(DENSE):
             c_bf = {}
             for lo, hi, copy in shares[a]:
-                base = max(b for b, e in splits[a] if b <= lo)
-                c_bf[lo] = keep.tile([P, (hi - lo) * J], BF16, name="c_bf%d_%d" % (a, lo), align_bytes=64)
-                interleave(copy, c_bf[lo][:], c_raw[a, base][:, :, lo - base : hi - base])
-            done = 0
+                base = max(start for start, end in c_loads[a] if start <= lo)
+                c_bf[lo] = keep.tile([P, (hi - lo) * J], BF16, name="c_bf%d_%d" % (a, lo), align_bytes=MX_ALIGN)
+                copy(woven(c_bf[lo][:]), by_planes(c_raw[a, base][:, :, lo - base : hi - base]))
             for lo, hi, copy in shares[a]:
                 nc.vector.quantize_mx(
                     out=c_codes[a][:, lo:hi].bitcast(E4M3), scales=c_scales[a][:, lo:hi], in_=c_bf[lo][:]
                 )
-                for g in range(done, hi // GROUP):
+                for g in range(lo // GROUP, hi // GROUP):
                     cols = slice(g * GROUP, (g + 1) * GROUP)
                     nc.tensor.matmul_mx(
                         out=acc[g][:],
@@ -162,7 +162,8 @@ def tile_list_hmix_none_kernel(tc, xT, w4_words, w4_scales, c, u, wgt, offs, out
                         start=False,
                         stop=(a == DENSE - 1),
                     )
-                done = hi // GROUP
-        for g in range(groups):
-            out_copy[g](res[g], acc[g][:])
-            out_queue[g].dma_start(out=out[:, g * GROUP : (g + 1) * GROUP], in_=res[g])
+
+        staged = c_raw[DENSE - 1, S - GROUP]
+        for g, copy in enumerate((sca, sca, vec, vec)):
+            copy(staged[:, g, :], acc[g][:])
+            nc.sync.dma_start(out=out[:, g * GROUP : (g + 1) * GROUP], in_=staged[:, g, :])

@@ -70,13 +70,14 @@ def tile_list_hmix_none_kernel(tc, xT, w4_words, w4_scales, c, u, wgt, offs, out
         for t in range(1, J):
             nc.sync.dma_start(out=xt[t][:], in_=x_planes[t])
         nc.sync.dma_start(out=u_raw[:], in_=u_rows)
-        nc.sync.dma_start(out=w4_sb[:].bitcast(I32), in_=w4_words[0].bitcast(I32))
         for q in range(4):
             nc.sync.dma_start(
                 out=w4_sc[32 * q : 32 * q + 4, :].bitcast(I32),
                 in_=w4_scales[0, 4 * q : 4 * q + 4, :].bitcast(I32),
             )
         for a in range(DENSE):
+            if a == DENSE - 1:
+                nc.sync.dma_start(out=w4_sb[:].bitcast(I32), in_=w4_words[0].bitcast(I32))
             for lo, hi in c_loads[a]:
                 nc.sync.dma_start(out=c_raw[a, lo][:], in_=c_rows[a, :, :, lo:hi])
 

@@ -66,12 +66,12 @@ def tile_list_hmix_none_kernel(tc, xT, w4_words, w4_scales, c, u, wgt, offs, out
         nc.vector.memset(w4_sc[:].bitcast(I32), 0)
         nc.sync.dma_start(out=xt[0][:], in_=x_planes[0])
         nc.sync.dma_start(offs_sb[:], offs)
-        nc.sync.dma_start(out=wgt_cut[:], in_=wgt.rearrange("(g r) (b c) -> r g b c", r=HEAD, c=SQUARE)[0])
+        nc.scalar.dma_start(out=wgt_cut[:], in_=wgt.rearrange("(g r) (b c) -> r g b c", r=HEAD, c=SQUARE)[0])
         for t in range(1, J):
             nc.sync.dma_start(out=xt[t][:], in_=x_planes[t])
         nc.sync.dma_start(out=u_raw[:], in_=u_rows)
         for q in range(4):
-            nc.sync.dma_start(
+            nc.scalar.dma_start(
                 out=w4_sc[32 * q : 32 * q + 4, :].bitcast(I32),
                 in_=w4_scales[0, 4 * q : 4 * q + 4, :].bitcast(I32),
             )

@@ -69,6 +69,8 @@ def tile_list_hmix_none_kernel(tc, xT, w4_words, w4_scales, c, u, wgt, offs, out
         nc.scalar.dma_start(out=wgt_cut[:], in_=wgt.rearrange("(g r) (b c) -> r g b c", r=HEAD, c=SQUARE)[0])
         for t in range(1, J):
             nc.sync.dma_start(out=xt[t][:], in_=x_planes[t])
+            if t == 2:
+                nc.sync.dma_start(out=w4_sb[:].bitcast(I32), in_=w4_words[0].bitcast(I32))
         nc.sync.dma_start(out=u_raw[:], in_=u_rows)
         for q in range(4):
             nc.scalar.dma_start(
@@ -76,8 +78,6 @@ def tile_list_hmix_none_kernel(tc, xT, w4_words, w4_scales, c, u, wgt, offs, out
                 in_=w4_scales[0, 4 * q : 4 * q + 4, :].bitcast(I32),
             )
         for a in range(DENSE):
-            if a == DENSE - 1:
-                nc.sync.dma_start(out=w4_sb[:].bitcast(I32), in_=w4_words[0].bitcast(I32))
             for lo, hi in c_loads[a]:
                 nc.sync.dma_start(out=c_raw[a, lo][:], in_=c_rows[a, :, :, lo:hi])
 
@@ -119,7 +119,8 @@ def tile_list_hmix_none_kernel(tc, xT, w4_words, w4_scales, c, u, wgt, offs, out
 
         groups = S // GROUP
         acc = [psum.tile([M, GROUP], F32, name="acc%d" % g) for g in range(groups)]
-        for g in range(groups):
+
+        def w4_pass(g):
             cols = slice(g * GROUP, (g + 1) * GROUP)
             nc.tensor.matmul_mx(
                 out=acc[g][:],
@@ -127,8 +128,20 @@ def tile_list_hmix_none_kernel(tc, xT, w4_words, w4_scales, c, u, wgt, offs, out
                 lhsT_scale=w4_sc[:],
                 rhs=x_codes[:, cols].bitcast(E4M3),
                 rhs_scale=x_scales[:, cols],
-                start=True,
+                start=False,
                 stop=False,
+            )
+
+        def dense_pass(a, g):
+            cols = slice(g * GROUP, (g + 1) * GROUP)
+            nc.tensor.matmul_mx(
+                out=acc[g][:],
+                lhsT=u_codes[:, a, :].bitcast(E4M3),
+                lhsT_scale=u_scales[:, a, :],
+                rhs=c_codes[a][:, cols].bitcast(E4M3),
+                rhs_scale=c_scales[a][:, cols],
+                start=(a == DENSE - 2),
+                stop=(a == DENSE - 1),
             )
 
         c_codes = [keep.tile([P, S], U32, name="c_codes%d" % a, align_bytes=MX_ALIGN) for a in range(DENSE)]
@@ -153,16 +166,11 @@ def tile_list_hmix_none_kernel(tc, xT, w4_words, w4_scales, c, u, wgt, offs, out
                     out=c_codes[a][:, lo:hi].bitcast(E4M3), scales=c_scales[a][:, lo:hi], in_=c_bf[lo][:]
                 )
                 for g in range(lo // GROUP, hi // GROUP):
-                    cols = slice(g * GROUP, (g + 1) * GROUP)
-                    nc.tensor.matmul_mx(
-                        out=acc[g][:],
-                        lhsT=u_codes[:, a, :].bitcast(E4M3),
-                        lhsT_scale=u_scales[:, a, :],
-                        rhs=c_codes[a][:, cols].bitcast(E4M3),
-                        rhs_scale=c_scales[a][:, cols],
-                        start=False,
-                        stop=(a == DENSE - 1),
-                    )
+                    if a > 0:
+                        dense_pass(a, g)
+                    if a == DENSE - 2:
+                        w4_pass(g)
+                        dense_pass(0, g)
 
         staged = c_raw[DENSE - 1, S - GROUP]
         for g, copy in enumerate((sca, sca, vec, vec)):

@@ -52,7 +52,7 @@ def tile_list_hmix_none_kernel(tc, xT, w4_words, w4_scales, c, u, wgt, offs, out
         w4_sb = keep.tile([P, 2 * M], U8, name="w4_sb", align_bytes=MX_ALIGN)
         w4_sc = keep.tile([P, M], U8, name="w4_sc", align_bytes=MX_ALIGN)
         xt = [keep.tile([P, T], F32, name="xt%d" % t, align_bytes=ROW_ALIGN) for t in range(J)]
-        c_loads = [[(lo, lo + (S >> a)) for lo in range(0, S, S >> a)] for a in range(DENSE)]
+        c_loads = [[(0, S)], [(0, S)], [(0, 256), (256, 384), (384, S)]]
         c_raw = {
             (a, lo): keep.tile([P, J, hi - lo], F32, name="c_raw%d_%d" % (a, lo), align_bytes=ROW_ALIGN)
             for a in range(DENSE)
@@ -69,15 +69,15 @@ def tile_list_hmix_none_kernel(tc, xT, w4_words, w4_scales, c, u, wgt, offs, out
         nc.scalar.dma_start(out=wgt_cut[:], in_=wgt.rearrange("(g r) (b c) -> r g b c", r=HEAD, c=SQUARE)[0])
         for t in range(1, J):
             nc.sync.dma_start(out=xt[t][:], in_=x_planes[t])
-            if t == 2:
-                nc.sync.dma_start(out=w4_sb[:].bitcast(I32), in_=w4_words[0].bitcast(I32))
-        nc.sync.dma_start(out=u_raw[:], in_=u_rows)
         for q in range(4):
             nc.scalar.dma_start(
                 out=w4_sc[32 * q : 32 * q + 4, :].bitcast(I32),
                 in_=w4_scales[0, 4 * q : 4 * q + 4, :].bitcast(I32),
             )
         for a in range(DENSE):
+            if a == DENSE - 1:
+                nc.sync.dma_start(out=u_raw[:], in_=u_rows)
+                nc.sync.dma_start(out=w4_sb[:].bitcast(I32), in_=w4_words[0].bitcast(I32))
             for lo, hi in c_loads[a]:
                 nc.sync.dma_start(out=c_raw[a, lo][:], in_=c_rows[a, :, :, lo:hi])
 
@@ -112,7 +112,7 @@ def tile_list_hmix_none_kernel(tc, xT, w4_words, w4_scales, c, u, wgt, offs, out
         u_codes = keep.tile([P, DENSE, M], U32, name="u_codes", align_bytes=MX_ALIGN)
         u_scales = keep.tile([P, DENSE, M], U8, name="u_scales", align_bytes=MX_ALIGN)
         u_bf = [keep.tile([P, M * J], BF16, name="u_bf%d" % a, align_bytes=MX_ALIGN) for a in range(DENSE)]
-        for a, copy in enumerate((sca, vec, sca)):
+        for a, copy in enumerate((vec, vec, sca)):
             copy(woven(u_bf[a][:]), by_planes(u_raw[:, a, :].rearrange("p (j n) -> p j n", j=J)))
         for a in range(DENSE):
             nc.vector.quantize_mx(out=u_codes[:, a, :].bitcast(E4M3), scales=u_scales[:, a, :], in_=u_bf[a][:])
@@ -128,7 +128,7 @@ def tile_list_hmix_none_kernel(tc, xT, w4_words, w4_scales, c, u, wgt, offs, out
                 lhsT_scale=w4_sc[:],
                 rhs=x_codes[:, cols].bitcast(E4M3),
                 rhs_scale=x_scales[:, cols],
-                start=False,
+                start=True,
                 stop=False,
             )
 
@@ -140,37 +140,43 @@ def tile_list_hmix_none_kernel(tc, xT, w4_words, w4_scales, c, u, wgt, offs, out
                 lhsT_scale=u_scales[:, a, :],
                 rhs=c_codes[a][:, cols].bitcast(E4M3),
                 rhs_scale=c_scales[a][:, cols],
-                start=(a == DENSE - 2),
+                start=False,
                 stop=(a == DENSE - 1),
             )
 
+        for g in range(groups):
+            w4_pass(g)
+
         c_codes = [keep.tile([P, S], U32, name="c_codes%d" % a, align_bytes=MX_ALIGN) for a in range(DENSE)]
         c_scales = [keep.tile([P, S], U8, name="c_scales%d" % a, align_bytes=MX_ALIGN) for a in range(DENSE)]
-        shares = []
         for a in range(DENSE):
-            shares.append([])
-            for i, (lo, hi) in enumerate(c_loads[a]):
-                if a < DENSE - 1 or hi == S:
+            if a < DENSE - 1:
+                shares = []
+                for lo, hi in c_loads[a]:
                     mid = (lo + hi) // 2
-                    shares[a].extend([(lo, mid, vec), (mid, hi, sca)])
-                else:
-                    shares[a].append((lo, hi, (sca, vec)[i % 2]))
-        for a in range(DENSE):
-            c_bf = {}
-            for lo, hi, copy in shares[a]:
+                    shares.extend([(lo, mid, vec), (mid, hi, sca)])
+                edges = [lo for lo, hi, copy in shares] + [S]
+            else:
+                shares = [(0, 128, vec), (128, 192, vec), (192, 256, sca), (256, 288, vec), (288, 384, sca), (384, 448, vec), (448, S, sca)]
+                edges = [0, 128, 256, 384, 448, S]
+            calls = list(zip(edges[:-1], edges[1:]))
+            c_bf = {
+                lo: keep.tile([P, (hi - lo) * J], BF16, name="c_bf%d_%d" % (a, lo), align_bytes=MX_ALIGN)
+                for lo, hi in calls
+            }
+            for lo, hi, copy in shares:
                 base = max(start for start, end in c_loads[a] if start <= lo)
-                c_bf[lo] = keep.tile([P, (hi - lo) * J], BF16, name="c_bf%d_%d" % (a, lo), align_bytes=MX_ALIGN)
-                copy(woven(c_bf[lo][:]), by_planes(c_raw[a, base][:, :, lo - base : hi - base]))
-            for lo, hi, copy in shares[a]:
+                first = max(start for start, end in calls if start <= lo)
+                copy(
+                    woven(c_bf[first][:, (lo - first) * J : (hi - first) * J]),
+                    by_planes(c_raw[a, base][:, :, lo - base : hi - base]),
+                )
+            for lo, hi in calls:
                 nc.vector.quantize_mx(
                     out=c_codes[a][:, lo:hi].bitcast(E4M3), scales=c_scales[a][:, lo:hi], in_=c_bf[lo][:]
                 )
                 for g in range(lo // GROUP, hi // GROUP):
-                    if a > 0:
-                        dense_pass(a, g)
-                    if a == DENSE - 2:
-                        w4_pass(g)
-                        dense_pass(0, g)
+                    dense_pass(a, g)
 
         staged = c_raw[DENSE - 1, S - GROUP]
         for g, copy in enumerate((sca, sca, vec, vec)):

@@ -112,8 +112,9 @@ def tile_list_hmix_none_kernel(tc, xT, w4_words, w4_scales, c, u, wgt, offs, out
         u_codes = keep.tile([P, DENSE, M], U32, name="u_codes", align_bytes=MX_ALIGN)
         u_scales = keep.tile([P, DENSE, M], U8, name="u_scales", align_bytes=MX_ALIGN)
         u_bf = [keep.tile([P, M * J], BF16, name="u_bf%d" % a, align_bytes=MX_ALIGN) for a in range(DENSE)]
-        for a, copy in enumerate((vec, vec, sca)):
-            copy(woven(u_bf[a][:]), by_planes(u_raw[:, a, :].rearrange("p (j n) -> p j n", j=J)))
+        for a, lo, hi, copy in ((0, 0, M, vec), (1, 0, M // 2, vec), (1, M // 2, M, sca), (2, 0, M, sca)):
+            planes = u_raw[:, a, :].rearrange("p (j n) -> p j n", j=J)
+            copy(woven(u_bf[a][:, lo * J : hi * J]), by_planes(planes[:, :, lo:hi]))
         for a in range(DENSE):
             nc.vector.quantize_mx(out=u_codes[:, a, :].bitcast(E4M3), scales=u_scales[:, a, :], in_=u_bf[a][:])
 
@@ -151,13 +152,10 @@ def tile_list_hmix_none_kernel(tc, xT, w4_words, w4_scales, c, u, wgt, offs, out
         c_scales = [keep.tile([P, S], U8, name="c_scales%d" % a, align_bytes=MX_ALIGN) for a in range(DENSE)]
         for a in range(DENSE):
             if a < DENSE - 1:
-                shares = []
-                for lo, hi in c_loads[a]:
-                    mid = (lo + hi) // 2
-                    shares.extend([(lo, mid, vec), (mid, hi, sca)])
-                edges = [lo for lo, hi, copy in shares] + [S]
+                shares = [(0, 128, vec), (128, 256, sca), (256, S, sca)] if a == 0 else [(0, 256, vec), (256, S, sca)]
+                edges = [0, S // 2, S]
             else:
-                shares = [(0, 128, vec), (128, 192, vec), (192, 256, sca), (256, 288, vec), (288, 384, sca), (384, 448, vec), (448, S, sca)]
+                shares = [(0, 128, vec), (128, 256, sca), (256, 288, vec), (288, 384, sca), (384, 448, vec), (448, S, sca)]
                 edges = [0, 128, 256, 384, 448, S]
             calls = list(zip(edges[:-1], edges[1:]))
             c_bf = {

@@ -155,23 +155,19 @@ def tile_list_hmix_none_kernel(tc, xT, w4_words, w4_scales, c, u, wgt, offs, out
                 shares = [(0, 128, vec), (128, 256, sca), (256, S, sca)] if a == 0 else [(0, 256, vec), (256, S, sca)]
                 edges = [0, S // 2, S]
             else:
-                shares = [(0, 128, vec), (128, 256, sca), (256, 288, vec), (288, 384, sca), (384, 448, vec), (448, S, sca)]
+                shares = [(0, 128, vec), (128, 256, sca), (256, 288, vec), (288, 384, sca), (384, 448, sca), (448, S, vec)]
                 edges = [0, 128, 256, 384, 448, S]
             calls = list(zip(edges[:-1], edges[1:]))
-            c_bf = {
-                lo: keep.tile([P, (hi - lo) * J], BF16, name="c_bf%d_%d" % (a, lo), align_bytes=MX_ALIGN)
-                for lo, hi in calls
-            }
+            c_bf = keep.tile([P, S * J], BF16, name="c_bf%d" % a, align_bytes=MX_ALIGN)
             for lo, hi, copy in shares:
                 base = max(start for start, end in c_loads[a] if start <= lo)
-                first = max(start for start, end in calls if start <= lo)
                 copy(
-                    woven(c_bf[first][:, (lo - first) * J : (hi - first) * J]),
+                    woven(c_bf[:, lo * J : hi * J]),
                     by_planes(c_raw[a, base][:, :, lo - base : hi - base]),
                 )
             for lo, hi in calls:
                 nc.vector.quantize_mx(
-                    out=c_codes[a][:, lo:hi].bitcast(E4M3), scales=c_scales[a][:, lo:hi], in_=c_bf[lo][:]
+                    out=c_codes[a][:, lo:hi].bitcast(E4M3), scales=c_scales[a][:, lo:hi], in_=c_bf[:, lo * J : hi * J]
                 )
                 for g in range(lo // GROUP, hi // GROUP):
                     dense_pass(a, g)

@@ -46,8 +46,8 @@ def tile_list_hmix_none_kernel(tc, xT, w4_words, w4_scales, c, u, wgt, offs, out
 
         offs_sb = lists.tile([P, S // HEAD], U16, name="offs_sb")
         wgt_sb = keep.tile([P, S], F32, name="wgt_sb", align_bytes=MX_ALIGN)
-        wgt_cut = keep.tile([P, SQUARE], F32, name="wgt_cut", align_bytes=MX_ALIGN)
-        wgt_turned = keep.tile([P, SQUARE], F32, name="wgt_turned", align_bytes=MX_ALIGN)
+        wgt_rows = keep.tile([P, S // 4], F32, name="wgt_rows", align_bytes=ROW_ALIGN)
+        wgt_turned = keep.tile([P, S // 4], F32, name="wgt_turned", align_bytes=MX_ALIGN)
         wgt_wide = keep.tile([P, S], F32, name="wgt_wide", align_bytes=MX_ALIGN)
         w4_sb = keep.tile([P, 2 * M], U8, name="w4_sb", align_bytes=MX_ALIGN)
         w4_sc = keep.tile([P, M], U8, name="w4_sc", align_bytes=MX_ALIGN)
@@ -63,10 +63,11 @@ def tile_list_hmix_none_kernel(tc, xT, w4_words, w4_scales, c, u, wgt, offs, out
         x_planes = xT.rearrange("(p j) t -> j p t", j=J)
         c_rows = c.rearrange("(a p j) n -> a p j n", p=P, j=J)
         u_rows = u.rearrange("(a p j) n -> p a (j n)", p=P, j=J)
-        nc.vector.memset(w4_sc[:].bitcast(I32), 0)
+        nc.vector.memset(wgt_rows[:], 0.0)
+        nc.gpsimd.memset(w4_sc[:].bitcast(I32), 0)
         nc.sync.dma_start(out=xt[0][:], in_=x_planes[0])
         nc.sync.dma_start(offs_sb[:], offs)
-        nc.scalar.dma_start(out=wgt_cut[:], in_=wgt.rearrange("(g r) (b c) -> r g b c", r=HEAD, c=SQUARE)[0])
+        nc.scalar.dma_start(out=wgt_rows[0:P:4, :], in_=wgt.rearrange("(g r) (q c) -> r g q c", r=HEAD, q=4)[0])
         for t in range(1, J):
             nc.sync.dma_start(out=xt[t][:], in_=x_planes[t])
         for q in range(4):
@@ -81,20 +82,23 @@ def tile_list_hmix_none_kernel(tc, xT, w4_words, w4_scales, c, u, wgt, offs, out
             for lo, hi in c_loads[a]:
                 nc.sync.dma_start(out=c_raw[a, lo][:], in_=c_rows[a, :, :, lo:hi])
 
-        nc.vector.transpose(wgt_turned[:], wgt_cut[:])
+        nc.vector.transpose(wgt_turned[:], wgt_rows[:])
         vec(
-            wgt_wide[:].rearrange("p (b h r) -> p b h r", h=2, r=HEAD),
-            wgt_turned[:].rearrange("p (h b o) -> p b h o", h=2, o=1).to_broadcast([P, S // SQUARE, 2, HEAD]),
+            wgt_wide[:].rearrange("p (q b h r) -> p q b h r", q=4, h=2, r=HEAD),
+            wgt_turned[:].rearrange("p (b h q r) -> p q b h r", h=2, q=4, r=4)[:, :, :, :, 0:1].to_broadcast([P, 4, 4, 2, HEAD]),
         )
         nc.vector.transpose(wgt_sb[:], wgt_wide[:])
 
         halves = S // HALF
-        picked = [keep.tile([P, J, HALF], F32, name="picked%d" % h) for h in range(halves)]
-        for t in range(J):
+        early = keep.tile([P, 2, S], F32, name="early")
+        late = [keep.tile([P, 2, HALF], F32, name="late%d" % h) for h in range(halves)]
+        for t in range(2):
+            nc.vector.tensor_tensor(early[:, t, :], xt[t][:].indirect(offs_sb[:]), wgt_sb[:], MULT)
+        for t in range(2):
             for h in range(halves):
                 nc.vector.tensor_tensor(
-                    picked[h][:, t, :],
-                    xt[t][:].indirect(offs_sb[:, h * HALF // HEAD : (h + 1) * HALF // HEAD]),
+                    late[h][:, t, :],
+                    xt[2 + t][:].indirect(offs_sb[:, h * HALF // HEAD : (h + 1) * HALF // HEAD]),
                     wgt_sb[:, h * HALF : (h + 1) * HALF],
                     MULT,
                 )
@@ -102,9 +106,10 @@ def tile_list_hmix_none_kernel(tc, xT, w4_words, w4_scales, c, u, wgt, offs, out
         x_codes = keep.tile([P, S], U32, name="x_codes", align_bytes=MX_ALIGN)
         x_scales = keep.tile([P, S], U8, name="x_scales", align_bytes=MX_ALIGN)
         x_bf = [keep.tile([P, HALF * J], BF16, name="x_bf%d" % h, align_bytes=MX_ALIGN) for h in range(halves)]
-        for first, engines in ((0, (sca, sca)), (2, (sca, vec))):
-            for h in range(halves):
-                engines[h](woven(x_bf[h][:])[:, :, first : first + 2, :], by_planes(picked[h][:, first : first + 2, :]))
+        for h in range(halves):
+            sca(woven(x_bf[h][:])[:, :, 0:2, :], by_planes(early[:, :, h * HALF : (h + 1) * HALF]))
+        for h, copy in enumerate((sca, vec)):
+            copy(woven(x_bf[h][:])[:, :, 2:J, :], by_planes(late[h][:]))
         for h in range(halves):
             cols = slice(h * HALF, (h + 1) * HALF)
             nc.vector.quantize_mx(out=x_codes[:, cols].bitcast(E4M3), scales=x_scales[:, cols], in_=x_bf[h][:])

@@ -24,8 +24,10 @@ GROUP = 128
 HALF = S // 2
 HEAD = 16
 SQUARE = 32
+QUADS = 4
 MX_ALIGN = 64
 ROW_ALIGN = 256
+MOVED_BY_SCALAR = 1536
 
 
 def woven(tile):
@@ -45,13 +47,15 @@ def tile_list_hmix_none_kernel(tc, xT, w4_words, w4_scales, c, u, wgt, offs, out
         vec, sca = nc.vector.tensor_copy, nc.scalar.copy
 
         offs_sb = lists.tile([P, S // HEAD], U16, name="offs_sb")
-        wgt_sb = keep.tile([P, S], F32, name="wgt_sb", align_bytes=MX_ALIGN)
-        wgt_rows = keep.tile([P, S // 4], F32, name="wgt_rows", align_bytes=ROW_ALIGN)
-        wgt_turned = keep.tile([P, S // 4], F32, name="wgt_turned", align_bytes=MX_ALIGN)
+        wgt_cut = keep.tile([P, SQUARE], F32, name="wgt_cut", align_bytes=MX_ALIGN)
+        wgt_turned = keep.tile([P, SQUARE], F32, name="wgt_turned", align_bytes=MX_ALIGN)
         wgt_wide = keep.tile([P, S], F32, name="wgt_wide", align_bytes=MX_ALIGN)
+        wgt_sb = keep.tile([P, S], F32, name="wgt_sb", align_bytes=MX_ALIGN)
         w4_sb = keep.tile([P, 2 * M], U8, name="w4_sb", align_bytes=MX_ALIGN)
         w4_sc = keep.tile([P, M], U8, name="w4_sc", align_bytes=MX_ALIGN)
-        xt = [keep.tile([P, T], F32, name="xt%d" % t, align_bytes=ROW_ALIGN) for t in range(J)]
+        w4_rows = keep.tile([4, QUADS, M // 4], I32, name="w4_rows", align_bytes=MX_ALIGN)
+        x_first = keep.tile([P, 2 * T], F32, name="x_first", align_bytes=ROW_ALIGN)
+        xt = [x_first] + [keep.tile([P, T], F32, name="xt%d" % t, align_bytes=ROW_ALIGN) for t in range(1, J)]
         c_loads = [[(0, S)], [(0, S)], [(0, 256), (256, 384), (384, S)]]
         c_raw = {
             (a, lo): keep.tile([P, J, hi - lo], F32, name="c_raw%d_%d" % (a, lo), align_bytes=ROW_ALIGN)
@@ -60,21 +64,16 @@ def tile_list_hmix_none_kernel(tc, xT, w4_words, w4_scales, c, u, wgt, offs, out
         }
         u_raw = keep.tile([P, DENSE, J * M], F32, name="u_raw", align_bytes=ROW_ALIGN)
 
-        x_planes = xT.rearrange("(p j) t -> j p t", j=J)
+        x_rows = xT.rearrange("(p j) t -> p (j t)", j=J)
         c_rows = c.rearrange("(a p j) n -> a p j n", p=P, j=J)
         u_rows = u.rearrange("(a p j) n -> p a (j n)", p=P, j=J)
-        nc.vector.memset(wgt_rows[:], 0.0)
         nc.gpsimd.memset(w4_sc[:].bitcast(I32), 0)
-        nc.sync.dma_start(out=xt[0][:], in_=x_planes[0])
+        nc.scalar.dma_start(out=wgt_cut[:], in_=wgt.rearrange("(g r) (b i) -> r g b i", r=HEAD, i=SQUARE)[0])
+        nc.scalar.dma_start(out=w4_rows[:], in_=w4_scales[0].bitcast(I32).rearrange("(q i) c -> i q c", q=QUADS))
+        nc.sync.dma_start(out=x_first[:], in_=x_rows[:, 0 : 2 * T])
         nc.sync.dma_start(offs_sb[:], offs)
-        nc.scalar.dma_start(out=wgt_rows[0:P:4, :], in_=wgt.rearrange("(g r) (q c) -> r g q c", r=HEAD, q=4)[0])
-        for t in range(1, J):
-            nc.sync.dma_start(out=xt[t][:], in_=x_planes[t])
-        for q in range(4):
-            nc.scalar.dma_start(
-                out=w4_sc[32 * q : 32 * q + 4, :].bitcast(I32),
-                in_=w4_scales[0, 4 * q : 4 * q + 4, :].bitcast(I32),
-            )
+        for t in range(2, J):
+            nc.sync.dma_start(out=xt[t][:], in_=x_rows[:, t * T : (t + 1) * T])
         for a in range(DENSE):
             if a == DENSE - 1:
                 nc.sync.dma_start(out=u_raw[:], in_=u_rows)
@@ -82,26 +81,36 @@ def tile_list_hmix_none_kernel(tc, xT, w4_words, w4_scales, c, u, wgt, offs, out
             for lo, hi in c_loads[a]:
                 nc.sync.dma_start(out=c_raw[a, lo][:], in_=c_rows[a, :, :, lo:hi])
 
-        nc.vector.transpose(wgt_turned[:], wgt_rows[:])
-        vec(
-            wgt_wide[:].rearrange("p (q b h r) -> p q b h r", q=4, h=2, r=HEAD),
-            wgt_turned[:].rearrange("p (b h q r) -> p q b h r", h=2, q=4, r=4)[:, :, :, :, 0:1].to_broadcast([P, 4, 4, 2, HEAD]),
+        nc.vector.transpose(wgt_turned[:], wgt_cut[:])
+        sca(
+            wgt_wide[:].rearrange("p (b h r) -> p b h r", h=2, r=HEAD),
+            wgt_turned[:].rearrange("p (h b) -> p b h", h=2).unsqueeze(3).to_broadcast([P, HEAD, 2, HEAD]),
         )
         nc.vector.transpose(wgt_sb[:], wgt_wide[:])
+        for q in range(QUADS):
+            move = nc.gpsimd.tensor_copy if q == 0 else vec
+            move(w4_sc[32 * q : 32 * q + 4, :].bitcast(I32), w4_rows[:, q, :])
 
         halves = S // HALF
         early = keep.tile([P, 2, S], F32, name="early")
-        late = [keep.tile([P, 2, HALF], F32, name="late%d" % h) for h in range(halves)]
-        for t in range(2):
-            nc.vector.tensor_tensor(early[:, t, :], xt[t][:].indirect(offs_sb[:]), wgt_sb[:], MULT)
-        for t in range(2):
-            for h in range(halves):
-                nc.vector.tensor_tensor(
-                    late[h][:, t, :],
-                    xt[2 + t][:].indirect(offs_sb[:, h * HALF // HEAD : (h + 1) * HALF // HEAD]),
-                    wgt_sb[:, h * HALF : (h + 1) * HALF],
-                    MULT,
-                )
+        late = keep.tile([P, 2, S], F32, name="late")
+
+        def gather_half(picked, plane, h):
+            nc.vector.tensor_tensor(
+                picked[:, h * HALF : (h + 1) * HALF],
+                plane[:].indirect(offs_sb[:, h * HALF // HEAD : (h + 1) * HALF // HEAD]),
+                wgt_sb[:, h * HALF : (h + 1) * HALF],
+                MULT,
+            )
+
+        sca(xt[1][:, 0:MOVED_BY_SCALAR], x_first[:, T : T + MOVED_BY_SCALAR])
+        vec(xt[1][:, MOVED_BY_SCALAR:T], x_first[:, T + MOVED_BY_SCALAR : 2 * T])
+        for h in range(halves):
+            gather_half(early[:, 0, :], xt[0], h)
+        nc.vector.tensor_tensor(early[:, 1, :], xt[1][:].indirect(offs_sb[:]), wgt_sb[:], MULT)
+        nc.vector.tensor_tensor(late[:, 0, :], xt[2][:].indirect(offs_sb[:]), wgt_sb[:], MULT)
+        for h in range(halves):
+            gather_half(late[:, 1, :], xt[3], h)
 
         x_codes = keep.tile([P, S], U32, name="x_codes", align_bytes=MX_ALIGN)
         x_scales = keep.tile([P, S], U8, name="x_scales", align_bytes=MX_ALIGN)
@@ -109,7 +118,7 @@ def tile_list_hmix_none_kernel(tc, xT, w4_words, w4_scales, c, u, wgt, offs, out
         for h in range(halves):
             sca(woven(x_bf[h][:])[:, :, 0:2, :], by_planes(early[:, :, h * HALF : (h + 1) * HALF]))
         for h, copy in enumerate((sca, vec)):
-            copy(woven(x_bf[h][:])[:, :, 2:J, :], by_planes(late[h][:]))
+            copy(woven(x_bf[h][:])[:, :, 2:J, :], by_planes(late[:, :, h * HALF : (h + 1) * HALF]))
         for h in range(halves):
             cols = slice(h * HALF, (h + 1) * HALF)
             nc.vector.quantize_mx(out=x_codes[:, cols].bitcast(E4M3), scales=x_scales[:, cols], in_=x_bf[h][:])
@@ -157,8 +166,8 @@ def tile_list_hmix_none_kernel(tc, xT, w4_words, w4_scales, c, u, wgt, offs, out
         c_scales = [keep.tile([P, S], U8, name="c_scales%d" % a, align_bytes=MX_ALIGN) for a in range(DENSE)]
         for a in range(DENSE):
             if a < DENSE - 1:
-                shares = [(0, 128, vec), (128, 256, sca), (256, S, sca)] if a == 0 else [(0, 256, vec), (256, S, sca)]
-                edges = [0, S // 2, S]
+                shares = [(0, 192, vec), (192, S, sca)] if a == 0 else [(0, 320, vec), (320, S, sca)]
+                edges = [0, S]
             else:
                 shares = [(0, 128, vec), (128, 256, sca), (256, 288, vec), (288, 384, sca), (384, 448, sca), (448, S, vec)]
                 edges = [0, 128, 256, 384, 448, S]
@@ -177,7 +186,10 @@ def tile_list_hmix_none_kernel(tc, xT, w4_words, w4_scales, c, u, wgt, offs, out
                 for g in range(lo // GROUP, hi // GROUP):
                     dense_pass(a, g)
 
-        staged = c_raw[DENSE - 1, S - GROUP]
-        for g, copy in enumerate((sca, sca, vec, vec)):
+        staged = c_raw[DENSE - 1, S - 2 * GROUP]
+        for g, copy in enumerate((sca, sca, sca, vec)):
             copy(staged[:, g, :], acc[g][:])
-            nc.sync.dma_start(out=out[:, g * GROUP : (g + 1) * GROUP], in_=staged[:, g, :])
+            if g == 1:
+                nc.sync.dma_start(out=out[:, 0 : 2 * GROUP], in_=staged[:, 0:2, :].rearrange("p g n -> p (g n)"))
+            elif g > 1:
+                nc.sync.dma_start(out=out[:, g * GROUP : (g + 1) * GROUP], in_=staged[:, g, :])

@@ -28,6 +28,7 @@ QUADS = 4
 MX_ALIGN = 64
 ROW_ALIGN = 256
 MOVED_BY_SCALAR = 1536
+PACKET = 4096
 
 
 def woven(tile):
@@ -70,7 +71,7 @@ def tile_list_hmix_none_kernel(tc, xT, w4_words, w4_scales, c, u, wgt, offs, out
         nc.gpsimd.memset(w4_sc[:].bitcast(I32), 0)
         nc.scalar.dma_start(out=wgt_cut[:], in_=wgt.rearrange("(g r) (b i) -> r g b i", r=HEAD, i=SQUARE)[0])
         nc.scalar.dma_start(out=w4_rows[:], in_=w4_scales[0].bitcast(I32).rearrange("(q i) c -> i q c", q=QUADS))
-        nc.sync.dma_start(out=x_first[:], in_=x_rows[:, 0 : 2 * T])
+        nc.sync.dma_start(out=x_first[:], in_=x_rows[:, 0 : 2 * T], max_dma_last_dim=PACKET)
         nc.sync.dma_start(offs_sb[:], offs)
         for t in range(2, J):
             nc.sync.dma_start(out=xt[t][:], in_=x_rows[:, t * T : (t + 1) * T])

@@ -83,11 +83,15 @@ def tile_list_hmix_none_kernel(tc, xT, w4_words, w4_scales, c, u, wgt, offs, out
                 nc.sync.dma_start(out=c_raw[a, lo][:], in_=c_rows[a, :, :, lo:hi])
 
         nc.vector.transpose(wgt_turned[:], wgt_cut[:])
-        sca(
-            wgt_wide[:].rearrange("p (b h r) -> p b h r", h=2, r=HEAD),
-            wgt_turned[:].rearrange("p (h b) -> p b h", h=2).unsqueeze(3).to_broadcast([P, HEAD, 2, HEAD]),
-        )
-        nc.vector.transpose(wgt_sb[:], wgt_wide[:])
+        for h in range(S // HALF):
+            cols = slice(h * HALF, (h + 1) * HALF)
+            blocks = HALF // SQUARE
+            turned = wgt_turned[:].rearrange("p (h b) -> p b h", h=2)[:, h * blocks : (h + 1) * blocks, :]
+            sca(
+                wgt_wide[:, cols].rearrange("p (b h r) -> p b h r", h=2, r=HEAD),
+                turned.unsqueeze(3).to_broadcast([P, blocks, 2, HEAD]),
+            )
+            nc.vector.transpose(wgt_sb[:, cols], wgt_wide[:, cols])
         for q in range(QUADS):
             move = nc.gpsimd.tensor_copy if q == 0 else vec
             move(w4_sc[32 * q : 32 * q + 4, :].bitcast(I32), w4_rows[:, q, :])
@@ -115,14 +119,12 @@ def tile_list_hmix_none_kernel(tc, xT, w4_words, w4_scales, c, u, wgt, offs, out
 
         x_codes = keep.tile([P, S], U32, name="x_codes", align_bytes=MX_ALIGN)
         x_scales = keep.tile([P, S], U8, name="x_scales", align_bytes=MX_ALIGN)
-        x_bf = [keep.tile([P, HALF * J], BF16, name="x_bf%d" % h, align_bytes=MX_ALIGN) for h in range(halves)]
-        for h in range(halves):
-            sca(woven(x_bf[h][:])[:, :, 0:2, :], by_planes(early[:, :, h * HALF : (h + 1) * HALF]))
+        x_bf = keep.tile([P, S * J], BF16, name="x_bf", align_bytes=MX_ALIGN)
+        sca(woven(x_bf[:])[:, :, 0:2, :], by_planes(early[:]))
         for h, copy in enumerate((sca, vec)):
-            copy(woven(x_bf[h][:])[:, :, 2:J, :], by_planes(late[:, :, h * HALF : (h + 1) * HALF]))
-        for h in range(halves):
             cols = slice(h * HALF, (h + 1) * HALF)
-            nc.vector.quantize_mx(out=x_codes[:, cols].bitcast(E4M3), scales=x_scales[:, cols], in_=x_bf[h][:])
+            copy(woven(x_bf[:, h * HALF * J : (h + 1) * HALF * J])[:, :, 2:J, :], by_planes(late[:, :, cols]))
+        nc.vector.quantize_mx(out=x_codes[:].bitcast(E4M3), scales=x_scales[:], in_=x_bf[:])
 
         u_codes = keep.tile([P, DENSE, M], U32, name="u_codes", align_bytes=MX_ALIGN)
         u_scales = keep.tile([P, DENSE, M], U8, name="u_scales", align_bytes=MX_ALIGN)

from contextlib import ExitStack

import concourse.mybir as mybir

FLOPS = 268435456

F32 = mybir.dt.float32
BF16 = mybir.dt.bfloat16
I32 = mybir.dt.int32
U32 = mybir.dt.uint32
U16 = mybir.dt.uint16
U8 = mybir.dt.uint8
E4M3 = mybir.dt.float8_e4m3fn_x4
E2M1 = mybir.dt.float4_e2m1fn_x4
MULT = mybir.AluOpType.mult

P = 128
J = 4
M = 128
T = 2048
S = 512
DENSE = 3
GROUP = 128
HALF = S // 2
HEAD = 16
SQUARE = 32
QUADS = 4
MX_ALIGN = 64
ROW_ALIGN = 256
MOVED_BY_SCALAR = 1536
PACKET = 4096


def woven(tile):
    return tile.rearrange("p (c i t) -> p c t i", i=4, t=J)


def by_planes(planes):
    return planes.rearrange("p t (c i) -> p c t i", i=4)


def tile_list_hmix_none_kernel(tc, xT, w4_words, w4_scales, c, u, wgt, offs, out):
    nc = tc.nc
    with ExitStack() as ctx:
        lists = ctx.enter_context(tc.tile_pool(name="lists", bufs=1))
        keep = ctx.enter_context(tc.tile_pool(name="keep", bufs=1))
        psum = ctx.enter_context(tc.psum_pool(name="psum", bufs=1))
        vec, sca = nc.vector.tensor_copy, nc.scalar.copy

        offs_sb = lists.tile([P, S // HEAD], U16, name="offs_sb")
        wgt_cut = keep.tile([P, SQUARE], F32, name="wgt_cut", align_bytes=MX_ALIGN)
        wgt_turned = keep.tile([P, SQUARE], F32, name="wgt_turned", align_bytes=MX_ALIGN)
        wgt_wide = keep.tile([P, S], F32, name="wgt_wide", align_bytes=MX_ALIGN)
        wgt_sb = keep.tile([P, S], F32, name="wgt_sb", align_bytes=MX_ALIGN)
        w4_sb = keep.tile([P, 2 * M], U8, name="w4_sb", align_bytes=MX_ALIGN)
        w4_sc = keep.tile([P, M], U8, name="w4_sc", align_bytes=MX_ALIGN)
        w4_rows = keep.tile([4, QUADS, M // 4], I32, name="w4_rows", align_bytes=MX_ALIGN)
        x_first = keep.tile([P, 2 * T], F32, name="x_first", align_bytes=ROW_ALIGN)
        xt = [x_first] + [keep.tile([P, T], F32, name="xt%d" % t, align_bytes=ROW_ALIGN) for t in range(1, J)]
        c_loads = [[(0, S)], [(0, S)], [(0, 256), (256, 384), (384, S)]]
        c_raw = {
            (a, lo): keep.tile([P, J, hi - lo], F32, name="c_raw%d_%d" % (a, lo), align_bytes=ROW_ALIGN)
            for a in range(DENSE)
            for lo, hi in c_loads[a]
        }
        u_raw = keep.tile([P, DENSE, J * M], F32, name="u_raw", align_bytes=ROW_ALIGN)

        x_rows = xT.rearrange("(p j) t -> p (j t)", j=J)
        c_rows = c.rearrange("(a p j) n -> a p j n", p=P, j=J)
        u_rows = u.rearrange("(a p j) n -> p a (j n)", p=P, j=J)
        nc.gpsimd.memset(w4_sc[:].bitcast(I32), 0)
        nc.scalar.dma_start(out=wgt_cut[:], in_=wgt.rearrange("(g r) (b i) -> r g b i", r=HEAD, i=SQUARE)[0])
        nc.scalar.dma_start(out=w4_rows[:], in_=w4_scales[0].bitcast(I32).rearrange("(q i) c -> i q c", q=QUADS))
        nc.sync.dma_start(out=x_first[:], in_=x_rows[:, 0 : 2 * T], max_dma_last_dim=PACKET)
        nc.sync.dma_start(offs_sb[:], offs)
        for t in range(2, J):
            nc.sync.dma_start(out=xt[t][:], in_=x_rows[:, t * T : (t + 1) * T])
        for a in range(DENSE):
            if a == DENSE - 1:
                nc.sync.dma_start(out=u_raw[:], in_=u_rows)
                nc.sync.dma_start(out=w4_sb[:].bitcast(I32), in_=w4_words[0].bitcast(I32))
            for lo, hi in c_loads[a]:
                nc.sync.dma_start(out=c_raw[a, lo][:], in_=c_rows[a, :, :, lo:hi])

        nc.vector.transpose(wgt_turned[:], wgt_cut[:])
        for h in range(S // HALF):
            cols = slice(h * HALF, (h + 1) * HALF)
            blocks = HALF // SQUARE
            turned = wgt_turned[:].rearrange("p (h b) -> p b h", h=2)[:, h * blocks : (h + 1) * blocks, :]
            sca(
                wgt_wide[:, cols].rearrange("p (b h r) -> p b h r", h=2, r=HEAD),
                turned.unsqueeze(3).to_broadcast([P, blocks, 2, HEAD]),
            )
            nc.vector.transpose(wgt_sb[:, cols], wgt_wide[:, cols])
        for q in range(QUADS):
            move = nc.gpsimd.tensor_copy if q == 0 else vec
            move(w4_sc[32 * q : 32 * q + 4, :].bitcast(I32), w4_rows[:, q, :])

        halves = S // HALF
        early = keep.tile([P, 2, S], F32, name="early")
        late = keep.tile([P, 2, S], F32, name="late")

        def gather_half(picked, plane, h):
            nc.vector.tensor_tensor(
                picked[:, h * HALF : (h + 1) * HALF],
                plane[:].indirect(offs_sb[:, h * HALF // HEAD : (h + 1) * HALF // HEAD]),
                wgt_sb[:, h * HALF : (h + 1) * HALF],
                MULT,
            )

        sca(xt[1][:, 0:MOVED_BY_SCALAR], x_first[:, T : T + MOVED_BY_SCALAR])
        vec(xt[1][:, MOVED_BY_SCALAR:T], x_first[:, T + MOVED_BY_SCALAR : 2 * T])
        for h in range(halves):
            gather_half(early[:, 0, :], xt[0], h)
        nc.vector.tensor_tensor(early[:, 1, :], xt[1][:].indirect(offs_sb[:]), wgt_sb[:], MULT)
        nc.vector.tensor_tensor(late[:, 0, :], xt[2][:].indirect(offs_sb[:]), wgt_sb[:], MULT)
        for h in range(halves):
            gather_half(late[:, 1, :], xt[3], h)

        x_codes = keep.tile([P, S], U32, name="x_codes", align_bytes=MX_ALIGN)
        x_scales = keep.tile([P, S], U8, name="x_scales", align_bytes=MX_ALIGN)
        x_bf = keep.tile([P, S * J], BF16, name="x_bf", align_bytes=MX_ALIGN)
        sca(woven(x_bf[:])[:, :, 0:2, :], by_planes(early[:]))
        for h, copy in enumerate((sca, vec)):
            cols = slice(h * HALF, (h + 1) * HALF)
            copy(woven(x_bf[:, h * HALF * J : (h + 1) * HALF * J])[:, :, 2:J, :], by_planes(late[:, :, cols]))
        nc.vector.quantize_mx(out=x_codes[:].bitcast(E4M3), scales=x_scales[:], in_=x_bf[:])

        u_codes = keep.tile([P, DENSE, M], U32, name="u_codes", align_bytes=MX_ALIGN)
        u_scales = keep.tile([P, DENSE, M], U8, name="u_scales", align_bytes=MX_ALIGN)
        u_bf = [keep.tile([P, M * J], BF16, name="u_bf%d" % a, align_bytes=MX_ALIGN) for a in range(DENSE)]
        for a, lo, hi, copy in ((0, 0, M, vec), (1, 0, M // 2, vec), (1, M // 2, M, sca), (2, 0, M, sca)):
            planes = u_raw[:, a, :].rearrange("p (j n) -> p j n", j=J)
            copy(woven(u_bf[a][:, lo * J : hi * J]), by_planes(planes[:, :, lo:hi]))
        for a in range(DENSE):
            nc.vector.quantize_mx(out=u_codes[:, a, :].bitcast(E4M3), scales=u_scales[:, a, :], in_=u_bf[a][:])

        groups = S // GROUP
        acc = [psum.tile([M, GROUP], F32, name="acc%d" % g) for g in range(groups)]

        def w4_pass(g):
            cols = slice(g * GROUP, (g + 1) * GROUP)
            nc.tensor.matmul_mx(
                out=acc[g][:],
                lhsT=w4_sb[:].bitcast(E2M1),
                lhsT_scale=w4_sc[:],
                rhs=x_codes[:, cols].bitcast(E4M3),
                rhs_scale=x_scales[:, cols],
                start=True,
                stop=False,
            )

        def dense_pass(a, g):
            cols = slice(g * GROUP, (g + 1) * GROUP)
            nc.tensor.matmul_mx(
                out=acc[g][:],
                lhsT=u_codes[:, a, :].bitcast(E4M3),
                lhsT_scale=u_scales[:, a, :],
                rhs=c_codes[a][:, cols].bitcast(E4M3),
                rhs_scale=c_scales[a][:, cols],
                start=False,
                stop=(a == DENSE - 1),
            )

        for g in range(groups):
            w4_pass(g)

        c_codes = [keep.tile([P, S], U32, name="c_codes%d" % a, align_bytes=MX_ALIGN) for a in range(DENSE)]
        c_scales = [keep.tile([P, S], U8, name="c_scales%d" % a, align_bytes=MX_ALIGN) for a in range(DENSE)]
        for a in range(DENSE):
            if a < DENSE - 1:
                shares = [(0, 192, vec), (192, S, sca)] if a == 0 else [(0, 320, vec), (320, S, sca)]
                edges = [0, S]
            else:
                shares = [(0, 128, vec), (128, 256, sca), (256, 288, vec), (288, 384, sca), (384, 448, sca), (448, S, vec)]
                edges = [0, 128, 256, 384, 448, S]
            calls = list(zip(edges[:-1], edges[1:]))
            c_bf = keep.tile([P, S * J], BF16, name="c_bf%d" % a, align_bytes=MX_ALIGN)
            for lo, hi, copy in shares:
                base = max(start for start, end in c_loads[a] if start <= lo)
                copy(
                    woven(c_bf[:, lo * J : hi * J]),
                    by_planes(c_raw[a, base][:, :, lo - base : hi - base]),
                )
            for lo, hi in calls:
                nc.vector.quantize_mx(
                    out=c_codes[a][:, lo:hi].bitcast(E4M3), scales=c_scales[a][:, lo:hi], in_=c_bf[:, lo * J : hi * J]
                )
                for g in range(lo // GROUP, hi // GROUP):
                    dense_pass(a, g)

        staged = c_raw[DENSE - 1, S - 2 * GROUP]
        for g, copy in enumerate((sca, sca, sca, vec)):
            copy(staged[:, g, :], acc[g][:])
            if g == 1:
                nc.sync.dma_start(out=out[:, 0 : 2 * GROUP], in_=staged[:, 0:2, :].rearrange("p g n -> p (g n)"))
            elif g > 1:
                nc.sync.dma_start(out=out[:, g * GROUP : (g + 1) * GROUP], in_=staged[:, g, :])
